import numpy as np, ml_dtypes
CORES = [2,3,6,7,58,59,62,63,114,115,118,119]
N = 12
NP, TK = 4, 256
def setup_inputs(rng):
    return {"x": rng.standard_normal((N, 128, TK), dtype=np.float32).astype(ml_dtypes.bfloat16), "w1": (rng.standard_normal((N, 128, 128), dtype=np.float32) / 8).astype(ml_dtypes.bfloat16), "w2": (rng.standard_normal((N, 128, NP * 128), dtype=np.float32) / 8).astype(ml_dtypes.bfloat16)}
def setup_inputs_big(rng):
    d = setup_inputs(rng)
    for k in ("x", "w1", "w2"): d[k] = (d[k].astype(np.float32) * 1024.0).astype(d[k].dtype)
    return d
def setup_inputs_small(rng):
    d = setup_inputs(rng)
    for k in ("x", "w1", "w2"): d[k] = (d[k].astype(np.float32) * (1 / 1024.0)).astype(d[k].dtype)
    return d
def setup_inputs_apart(rng):
    d = setup_inputs(rng)
    f = (10.0 ** rng.permutation(np.linspace(-1.5, 1.5, N))).astype(np.float32).reshape(N, 1, 1)
    for k in ("x", "w1", "w2"): d[k] = (d[k].astype(np.float32) * f).astype(d[k].dtype)
    return d
def reference(x, w1, w2):
    X, W1, W2 = x.astype(np.float64), w1.astype(np.float64), w2.astype(np.float64)
    h = [np.maximum(W1[p].T @ X[p], 0.0) for p in range(NP)]
    y = np.full((N, 128, TK), np.nan)
    for q in range(NP, N):
        y[q] = sum(W2[q][:, 128 * p:128 * p + 128].T @ h[p] for p in range(NP))
    return {"y": y.astype(ml_dtypes.bfloat16 if x.dtype != np.float64 else np.float64)}

@@ -1,0 +1,209 @@
+from concourse.bass import DstId, RemoteDMATransfer
+from concourse.mybir import AluOpType
+
+NP_, TK, D = 4, 256, 128
+KSPLIT = 4
+
+SCRATCH = {
+    "xs":   ("sbuf", [128, TK], "bfloat16"),
+    "w1s":  ("sbuf", [128, D], "bfloat16"),
+    "zero": ("sbuf", [128, TK], "float32"),
+    "hs":   ("sbuf", [128, TK], "bfloat16"),
+    "hin":  ("sbuf", [128, NP_ * TK], "bfloat16"),
+    "w2s":  ("sbuf", [128, NP_ * D], "bfloat16"),
+    "wsib": ("sbuf", [128, NP_ * D], "bfloat16"),
+    "sb":   ("sbuf", [128, 3 * TK], "bfloat16"),
+    "rb":   ("sbuf", [128, 3 * TK], "bfloat16"),
+    "ysb":  ("sbuf", [128, TK], "bfloat16"),
+    "ps0":  ("psum", [128, 512], "float32"),
+    "ps1":  ("psum", [128, 512], "float32"),
+    "ps2":  ("psum", [128, 512], "float32"),
+    "ps3":  ("psum", [128, 512], "float32"),
+    "pt0":  ("psum", [128, 512], "float32"),
+    "pt1":  ("psum", [128, 512], "float32"),
+}
+SEMAPHORES = (["lx", "lw1", "zs", "m1", "hr", "sent", "lw", "warr", "st"]
+              + ["ha%d" % i for i in range(4)] + ["pm%d" % i for i in range(4)]
+              + ["cp%d" % i for i in range(1, 4)] + ["pa%d" % i for i in range(1, 4)]
+              + ["ad%d" % i for i in range(4)])
+
+
+def _engines(mask):
+    return [e for e in range(mask.bit_length()) if (mask >> e) & 1]
+
+
+def _mask(engs):
+    m = 0
+    for e in engs:
+        m |= 1 << e
+    return m
+
+
+def _split(engs, n):
+    size = 1
+    while size * 2 * n <= len(engs):
+        size *= 2
+    sizes = [size] * n
+    for i in range(n - 1, -1, -1):
+        if sum(sizes) + sizes[i] <= len(engs):
+            sizes[i] *= 2
+    out, at = [], 0
+    for s in sizes:
+        out.append(engs[at:at + s])
+        at += s
+    return out
+
+
+def _plan(T, topo):
+    cores = list(T.cores)
+    P, Q = cores[:NP_], cores[NP_:]
+    chips = []
+    for c in Q:
+        if topo.chip(c) not in chips:
+            chips.append(topo.chip(c))
+    part, team = {}, {}
+    for ch in chips:
+        qs = [c for c in Q if topo.chip(c) == ch]
+        dies = sorted(set(topo.die(c) for c in qs))
+        qd = dict((d, [c for c in qs if topo.die(c) == d]) for d in dies)
+        pd = dict((d, [p for p in range(NP_) if topo.die(P[p]) == d]) for d in dies)
+        for d in dies:
+            for i, c in enumerate(qd[d]):
+                if KSPLIT == 4:
+                    part[c], team[c] = [pd[d][i]], qs
+                elif KSPLIT == 2:
+                    part[c], team[c] = pd[d], [qd[e][i] for e in dies]
+                else:
+                    part[c], team[c] = list(range(NP_)), [c]
+        for c in qs:
+            assert sorted(p for m in team[c] for p in part[m]) == list(range(NP_))
+    return P, Q, chips, part, team
+
+
+def _dst(topo, c):
+    rid, pid, _ = topo.addr(c)
+    return DstId(rid=rid, pnc=pid)
+
+
+def _program_p(g, core, T, topo, p, Q, chips, part):
+    s = T.sem
+    g.sync.dma_start(T.xs[:], T.x[:]).then_inc(s.lx, 16)
+    g.scalar.dma_start(T.w1s[:], T.w1[:]).then_inc(s.lw1, 16)
+    g.vector.memset(T.zero[:], 0.0).then_inc(s.zs, 1)
+
+    g.tensor.wait_ge(s.lw1, 16)
+    g.tensor.wait_ge(s.lx, 16)
+    g.tensor.matmul(T.ps0[:, 0:TK], T.w1s[:], T.xs[:], True, True).then_inc(s.m1, 1)
+
+    g.vector.wait_ge(s.zs, 1)
+    g.vector.wait_ge(s.m1, 1)
+    g.vector.tensor_tensor(T.hs[:], T.ps0[:, 0:TK], T.zero[:], AluOpType.max).then_inc(s.hr, 1)
+
+    takers = [[c for c in Q if topo.chip(c) == ch and p in part[c]] for ch in chips]
+    common = -1
+    for cs in takers:
+        for c in cs:
+            assert topo.may_write(core, c)
+            common &= topo.mask(core, c)
+    groups = _split(_engines(common), len(chips))
+    transfers, total = [], 0
+    for cs, engs in zip(takers, groups):
+        slot = part[cs[0]].index(p)
+        assert all(part[c].index(p) == slot for c in cs)
+        transfers.append(RemoteDMATransfer(
+            dst_ids=[_dst(topo, c) for c in cs], dma_engine_mask=_mask(engs), remote_sem=s["ha%d" % slot],
+            srcs=[T.hs[:]], dsts=[T.hin[:, slot * TK:(slot + 1) * TK] for c in cs]))
+        total += len(engs)
+    g.wait_ge(s.hr, 1)
+    g.remote_dma_fused(transfers, local_sem=s.sent)
+    g.wait_ge(s.sent, total)
+    return len(groups[0])
+
+
+def _program_q(g, core, T, topo, part, team, h_inc):
+    s = T.sem
+    mine, tm = part[core], team[core]
+    G, nS, ti = len(tm), len(part[core]), team[core].index(core)
+    mate = [tm[(ti + d) % G] for d in range(G)]
+
+    g.sync.dma_start(T.w2s[:], T.w2[:]).then_inc(s.lw, 16)
+
+    sent = 0
+    if G > 1:
+        full = -1
+        for d in range(1, G):
+            full &= topo.mask(core, mate[d])
+        groups = _split(_engines(full), (G - 1) * nS)
+        transfers = []
+        for d in range(1, G):
+            for k, p in enumerate(part[mate[d]]):
+                engs = groups[(d - 1) * nS + k]
+                at = ((G - d - 1) * nS + k) * D
+                transfers.append(RemoteDMATransfer(
+                    dst_ids=[_dst(topo, mate[d])], dma_engine_mask=_mask(engs), remote_sem=s.warr,
+                    srcs=[T.w2s[:, p * D:(p + 1) * D]], dsts=[T.wsib[:, at:at + D]]))
+                sent += len(engs)
+        w_inc = sent
+        g.wait_ge(s.lw, 16)
+        g.remote_dma_fused(transfers, local_sem=s.sent)
+        for d in range(1, G):
+            rid, pid, _ = topo.addr(mate[d])
+            m = topo.mask(core, mate[d])
+            g.wait_ge(s["cp%d" % d], 1)
+            g.remote_dma(out_ap=T.rb[:, (G - d - 1) * TK:(G - d) * TK], in_ap=T.sb[:, (d - 1) * TK:d * TK],
+                         remote_sem=s["pa%d" % (G - d)], local_sem=s.sent, pid=pid, routing_id=rid,
+                         dma_engine_mask=m)
+            sent += len(_engines(m))
+        g.wait_ge(s.sent, sent)
+
+    ps = [T.ps0, T.ps1, T.ps2, T.ps3]
+    waited = set()
+    for d in list(range(1, G)) + [0]:
+        if d == 0:
+            g.tensor.wait_ge(s.lw, 16)
+        elif d == 1:
+            g.tensor.wait_ge(s.warr, w_inc)
+        for k, p in enumerate(mine):
+            if k not in waited:
+                g.tensor.wait_ge(s["ha%d" % k], h_inc)
+                waited.add(k)
+            at = ((d - 1) * nS + k) * D
+            w = T.w2s[:, p * D:(p + 1) * D] if d == 0 else T.wsib[:, at:at + D]
+            mm = g.tensor.matmul(ps[d][:, 0:TK], w, T.hin[:, k * TK:(k + 1) * TK], k == 0, k == nS - 1)
+        mm.then_inc(s["pm%d" % d], 1)
+
+    for d in range(1, G):
+        g.vector.wait_ge(s["pm%d" % d], 1)
+        g.vector.tensor_copy(T.sb[:, (d - 1) * TK:d * TK], ps[d][:, 0:TK]).then_inc(s["cp%d" % d], 1)
+    g.vector.wait_ge(s.pm0, 1)
+    cur, tmp = T.ps0[:, 0:TK], [T.pt0, T.pt1]
+    if G == 1:
+        g.vector.tensor_copy(T.ysb[:], cur).then_inc(s.ad0, 1)
+        last = s.ad0
+    for i, off in enumerate(range(G - 1, 0, -1)):
+        out = T.ysb[:] if off == 1 else tmp[i][:, 0:TK]
+        g.vector.wait_ge(s["pa%d" % off], len(_engines(topo.mask(mate[off], core))))
+        if i:
+            g.vector.wait_ge(last, 1)
+        last = s["ad%d" % i]
+        g.vector.tensor_tensor(out, cur, T.rb[:, (off - 1) * TK:off * TK], AluOpType.add).then_inc(last, 1)
+        cur = out
+
+    g.sync.wait_ge(last, 1)
+    g.sync.dma_start(T.y[:], T.ysb[:]).then_inc(s.st, 16)
+    g.sync.wait_ge(s.st, 16)
+
+
+def rank_program(g, core, T, topo):
+    rank = T.rank_of(core)
+    if rank is None:
+        return
+    P, Q, chips, part, team = _plan(T, topo)
+    if rank < NP_:
+        _program_p(g, core, T, topo, rank, Q, chips, part)
+    else:
+        common = -1
+        for c in Q:
+            common &= topo.mask(P[0], c)
+        h_inc = len(_split(_engines(common), len(chips))[0])
+        _program_q(g, core, T, topo, part, team, h_inc)

@@ -2,7 +2,6 @@ from concourse.bass import DstId, RemoteDMATransfer
 from concourse.mybir import AluOpType
 
 NP_, TK, D = 4, 256, 128
-KSPLIT = 4
 
 SCRATCH = {
     "xs":   ("sbuf", [128, TK], "bfloat16"),
@@ -11,21 +10,15 @@ SCRATCH = {
     "hs":   ("sbuf", [128, TK], "bfloat16"),
     "hin":  ("sbuf", [128, NP_ * TK], "bfloat16"),
     "w2s":  ("sbuf", [128, NP_ * D], "bfloat16"),
-    "wsib": ("sbuf", [128, NP_ * D], "bfloat16"),
-    "sb":   ("sbuf", [128, 3 * TK], "bfloat16"),
-    "rb":   ("sbuf", [128, 3 * TK], "bfloat16"),
+    "wsib": ("sbuf", [128, D], "bfloat16"),
+    "sb":   ("sbuf", [128, TK], "bfloat16"),
+    "rb":   ("sbuf", [128, TK], "bfloat16"),
     "ysb":  ("sbuf", [128, TK], "bfloat16"),
     "ps0":  ("psum", [128, 512], "float32"),
     "ps1":  ("psum", [128, 512], "float32"),
-    "ps2":  ("psum", [128, 512], "float32"),
-    "ps3":  ("psum", [128, 512], "float32"),
-    "pt0":  ("psum", [128, 512], "float32"),
-    "pt1":  ("psum", [128, 512], "float32"),
 }
-SEMAPHORES = (["lx", "lw1", "zs", "m1", "hr", "sent", "lw", "warr", "st"]
-              + ["ha%d" % i for i in range(4)] + ["pm%d" % i for i in range(4)]
-              + ["cp%d" % i for i in range(1, 4)] + ["pa%d" % i for i in range(1, 4)]
-              + ["ad%d" % i for i in range(4)])
+SEMAPHORES = (["lx", "lw1", "zs", "m1", "hr", "sent", "lw", "warr", "st", "pm0", "pm1", "cp", "pa", "fin"]
+              + ["ha%d" % i for i in range(NP_)])
 
 
 def _engines(mask):
@@ -43,15 +36,7 @@ def _split(engs, n):
     size = 1
     while size * 2 * n <= len(engs):
         size *= 2
-    sizes = [size] * n
-    for i in range(n - 1, -1, -1):
-        if sum(sizes) + sizes[i] <= len(engs):
-            sizes[i] *= 2
-    out, at = [], 0
-    for s in sizes:
-        out.append(engs[at:at + s])
-        at += s
-    return out
+    return [engs[i * size:(i + 1) * size] for i in range(n)]
 
 
 def _plan(T, topo):
@@ -61,23 +46,14 @@ def _plan(T, topo):
     for c in Q:
         if topo.chip(c) not in chips:
             chips.append(topo.chip(c))
-    part, team = {}, {}
+    takes, team = {}, {}
     for ch in chips:
         qs = [c for c in Q if topo.chip(c) == ch]
-        dies = sorted(set(topo.die(c) for c in qs))
-        qd = dict((d, [c for c in qs if topo.die(c) == d]) for d in dies)
-        pd = dict((d, [p for p in range(NP_) if topo.die(P[p]) == d]) for d in dies)
-        for d in dies:
-            for i, c in enumerate(qd[d]):
-                if KSPLIT == 4:
-                    part[c], team[c] = [pd[d][i]], qs
-                elif KSPLIT == 2:
-                    part[c], team[c] = pd[d], [qd[e][i] for e in dies]
-                else:
-                    part[c], team[c] = list(range(NP_)), [c]
-        for c in qs:
-            assert sorted(p for m in team[c] for p in part[m]) == list(range(NP_))
-    return P, Q, chips, part, team
+        for d in sorted(set(topo.die(c) for c in qs)):
+            for p, c in zip([p for p in range(NP_) if topo.die(P[p]) == d], [c for c in qs if topo.die(c) == d]):
+                takes[c], team[c] = p, qs
+        assert sorted(takes[c] for c in qs) == list(range(NP_))
+    return P, Q, chips, takes, team
 
 
 def _dst(topo, c):
@@ -85,7 +61,14 @@ def _dst(topo, c):
     return DstId(rid=rid, pnc=pid)
 
 
-def _program_p(g, core, T, topo, p, Q, chips, part):
+def _h_groups(topo, src, Q, chips):
+    common = -1
+    for c in Q:
+        common &= topo.mask(src, c)
+    return _split(_engines(common), len(chips))
+
+
+def _program_p(g, core, T, topo, p, Q, chips, takes):
     s = T.sem
     g.sync.dma_start(T.xs[:], T.x[:]).then_inc(s.lx, 16)
     g.scalar.dma_start(T.w1s[:], T.w1[:]).then_inc(s.lw1, 16)
@@ -99,97 +82,71 @@ def _program_p(g, core, T, topo, p, Q, chips, part):
     g.vector.wait_ge(s.m1, 1)
     g.vector.tensor_tensor(T.hs[:], T.ps0[:, 0:TK], T.zero[:], AluOpType.max).then_inc(s.hr, 1)
 
-    takers = [[c for c in Q if topo.chip(c) == ch and p in part[c]] for ch in chips]
-    common = -1
-    for cs in takers:
-        for c in cs:
-            assert topo.may_write(core, c)
-            common &= topo.mask(core, c)
-    groups = _split(_engines(common), len(chips))
     transfers, total = [], 0
-    for cs, engs in zip(takers, groups):
-        slot = part[cs[0]].index(p)
-        assert all(part[c].index(p) == slot for c in cs)
+    for ch, engs in zip(chips, _h_groups(topo, core, Q, chips)):
+        (c,) = [c for c in Q if topo.chip(c) == ch and takes[c] == p]
+        assert topo.may_write(core, c)
         transfers.append(RemoteDMATransfer(
-            dst_ids=[_dst(topo, c) for c in cs], dma_engine_mask=_mask(engs), remote_sem=s["ha%d" % slot],
-            srcs=[T.hs[:]], dsts=[T.hin[:, slot * TK:(slot + 1) * TK] for c in cs]))
+            dst_ids=[_dst(topo, c)], dma_engine_mask=_mask(engs), remote_sem=s.ha0,
+            srcs=[T.hs[:]], dsts=[T.hin[:, 0:TK]]))
         total += len(engs)
     g.wait_ge(s.hr, 1)
     g.remote_dma_fused(transfers, local_sem=s.sent)
     g.wait_ge(s.sent, total)
-    return len(groups[0])
 
 
-def _program_q(g, core, T, topo, part, team, h_inc):
+def _program_q(g, core, T, topo, takes, team, h_inc):
     s = T.sem
-    mine, tm = part[core], team[core]
-    G, nS, ti = len(tm), len(part[core]), team[core].index(core)
-    mate = [tm[(ti + d) % G] for d in range(G)]
+    near = [c for c in team[core] if topo.die(c) == topo.die(core)]
+    far = [c for c in team[core] if topo.die(c) != topo.die(core)]
+    (partner,) = [c for c in near if c != core]
+    me_p = takes[core]
+
+    def tile(p):
+        return T.w2s[:, p * D:(p + 1) * D]
+
+    def slot(k):
+        return T.hin[:, k * TK:(k + 1) * TK]
 
     g.sync.dma_start(T.w2s[:], T.w2[:]).then_inc(s.lw, 16)
 
-    sent = 0
-    if G > 1:
-        full = -1
-        for d in range(1, G):
-            full &= topo.mask(core, mate[d])
-        groups = _split(_engines(full), (G - 1) * nS)
-        transfers = []
-        for d in range(1, G):
-            for k, p in enumerate(part[mate[d]]):
-                engs = groups[(d - 1) * nS + k]
-                at = ((G - d - 1) * nS + k) * D
-                transfers.append(RemoteDMATransfer(
-                    dst_ids=[_dst(topo, mate[d])], dma_engine_mask=_mask(engs), remote_sem=s.warr,
-                    srcs=[T.w2s[:, p * D:(p + 1) * D]], dsts=[T.wsib[:, at:at + D]]))
-                sent += len(engs)
-        w_inc = sent
-        g.wait_ge(s.lw, 16)
-        g.remote_dma_fused(transfers, local_sem=s.sent)
-        for d in range(1, G):
-            rid, pid, _ = topo.addr(mate[d])
-            m = topo.mask(core, mate[d])
-            g.wait_ge(s["cp%d" % d], 1)
-            g.remote_dma(out_ap=T.rb[:, (G - d - 1) * TK:(G - d) * TK], in_ap=T.sb[:, (d - 1) * TK:d * TK],
-                         remote_sem=s["pa%d" % (G - d)], local_sem=s.sent, pid=pid, routing_id=rid,
-                         dma_engine_mask=m)
-            sent += len(_engines(m))
-        g.wait_ge(s.sent, sent)
+    rid, pid, _ = topo.addr(partner)
+    pmask = topo.mask(core, partner)
+    n_p = len(_engines(pmask))
+    fmask = -1
+    for c in far:
+        fmask &= topo.mask(core, c)
+    n_f = len(_engines(fmask))
+    g.wait_ge(s.lw, 16)
+    g.remote_dma(out_ap=T.wsib[:], in_ap=tile(takes[partner]), remote_sem=s.warr, local_sem=s.sent,
+                 pid=pid, routing_id=rid, dma_engine_mask=pmask)
+    k = 1 + near.index(core)
+    g.wait_ge(s.ha0, h_inc)
+    g.remote_dma_fused([RemoteDMATransfer(
+        dst_ids=[_dst(topo, c) for c in far], dma_engine_mask=fmask, remote_sem=s["ha%d" % k],
+        srcs=[slot(0)], dsts=[slot(k) for c in far])], local_sem=s.sent)
+    g.wait_ge(s.cp, 1)
+    g.remote_dma(out_ap=T.rb[:], in_ap=T.sb[:], remote_sem=s.pa, local_sem=s.sent,
+                 pid=pid, routing_id=rid, dma_engine_mask=pmask)
+    g.wait_ge(s.sent, 2 * n_p + n_f)
 
-    ps = [T.ps0, T.ps1, T.ps2, T.ps3]
-    waited = set()
-    for d in list(range(1, G)) + [0]:
-        if d == 0:
-            g.tensor.wait_ge(s.lw, 16)
-        elif d == 1:
-            g.tensor.wait_ge(s.warr, w_inc)
-        for k, p in enumerate(mine):
-            if k not in waited:
-                g.tensor.wait_ge(s["ha%d" % k], h_inc)
-                waited.add(k)
-            at = ((d - 1) * nS + k) * D
-            w = T.w2s[:, p * D:(p + 1) * D] if d == 0 else T.wsib[:, at:at + D]
-            mm = g.tensor.matmul(ps[d][:, 0:TK], w, T.hin[:, k * TK:(k + 1) * TK], k == 0, k == nS - 1)
-        mm.then_inc(s["pm%d" % d], 1)
+    g.tensor.wait_ge(s.warr, len(_engines(topo.mask(partner, core))))
+    g.tensor.wait_ge(s.ha0, h_inc)
+    g.tensor.matmul(T.ps1[:, 0:TK], T.wsib[:], slot(0), True, True).then_inc(s.pm1, 1)
+    g.tensor.wait_ge(s.lw, 16)
+    g.tensor.matmul(T.ps0[:, 0:TK], tile(me_p), slot(0), True, False)
+    for i, c in enumerate(far):
+        g.tensor.wait_ge(s["ha%d" % (1 + i)], len(_engines(topo.mask(c, core))))
+        mm = g.tensor.matmul(T.ps0[:, 0:TK], tile(takes[c]), slot(1 + i), False, i == len(far) - 1)
+    mm.then_inc(s.pm0, 1)
 
-    for d in range(1, G):
-        g.vector.wait_ge(s["pm%d" % d], 1)
-        g.vector.tensor_copy(T.sb[:, (d - 1) * TK:d * TK], ps[d][:, 0:TK]).then_inc(s["cp%d" % d], 1)
+    g.vector.wait_ge(s.pm1, 1)
+    g.vector.tensor_copy(T.sb[:], T.ps1[:, 0:TK]).then_inc(s.cp, 1)
+    g.vector.wait_ge(s.pa, len(_engines(topo.mask(partner, core))))
     g.vector.wait_ge(s.pm0, 1)
-    cur, tmp = T.ps0[:, 0:TK], [T.pt0, T.pt1]
-    if G == 1:
-        g.vector.tensor_copy(T.ysb[:], cur).then_inc(s.ad0, 1)
-        last = s.ad0
-    for i, off in enumerate(range(G - 1, 0, -1)):
-        out = T.ysb[:] if off == 1 else tmp[i][:, 0:TK]
-        g.vector.wait_ge(s["pa%d" % off], len(_engines(topo.mask(mate[off], core))))
-        if i:
-            g.vector.wait_ge(last, 1)
-        last = s["ad%d" % i]
-        g.vector.tensor_tensor(out, cur, T.rb[:, (off - 1) * TK:off * TK], AluOpType.add).then_inc(last, 1)
-        cur = out
+    g.vector.tensor_tensor(T.ysb[:], T.ps0[:, 0:TK], T.rb[:], AluOpType.add).then_inc(s.fin, 1)
 
-    g.sync.wait_ge(last, 1)
+    g.sync.wait_ge(s.fin, 1)
     g.sync.dma_start(T.y[:], T.ysb[:]).then_inc(s.st, 16)
     g.sync.wait_ge(s.st, 16)
 
@@ -198,12 +155,9 @@ def rank_program(g, core, T, topo):
     rank = T.rank_of(core)
     if rank is None:
         return
-    P, Q, chips, part, team = _plan(T, topo)
+    P, Q, chips, takes, team = _plan(T, topo)
     if rank < NP_:
-        _program_p(g, core, T, topo, rank, Q, chips, part)
+        _program_p(g, core, T, topo, rank, Q, chips, takes)
     else:
-        common = -1
-        for c in Q:
-            common &= topo.mask(P[0], c)
-        h_inc = len(_split(_engines(common), len(chips))[0])
-        _program_q(g, core, T, topo, part, team, h_inc)
+        h_inc = len(_h_groups(topo, P[takes[core]], Q, chips)[0])
+        _program_q(g, core, T, topo, takes, team, h_inc)

from concourse.bass import DstId, RemoteDMATransfer
from concourse.mybir import AluOpType

NP_, TK, D = 4, 256, 128

SCRATCH = {
    "xs":   ("sbuf", [128, TK], "bfloat16"),
    "w1s":  ("sbuf", [128, D], "bfloat16"),
    "zero": ("sbuf", [128, TK], "float32"),
    "hs":   ("sbuf", [128, TK], "bfloat16"),
    "hin":  ("sbuf", [128, NP_ * TK], "bfloat16"),
    "w2s":  ("sbuf", [128, NP_ * D], "bfloat16"),
    "wsib": ("sbuf", [128, D], "bfloat16"),
    "sb":   ("sbuf", [128, TK], "bfloat16"),
    "rb":   ("sbuf", [128, TK], "bfloat16"),
    "ysb":  ("sbuf", [128, TK], "bfloat16"),
    "ps0":  ("psum", [128, 512], "float32"),
    "ps1":  ("psum", [128, 512], "float32"),
}
SEMAPHORES = (["lx", "lw1", "zs", "m1", "hr", "sent", "lw", "warr", "st", "pm0", "pm1", "cp", "pa", "fin"]
              + ["ha%d" % i for i in range(NP_)])


def _engines(mask):
    return [e for e in range(mask.bit_length()) if (mask >> e) & 1]


def _mask(engs):
    m = 0
    for e in engs:
        m |= 1 << e
    return m


def _split(engs, n):
    size = 1
    while size * 2 * n <= len(engs):
        size *= 2
    return [engs[i * size:(i + 1) * size] for i in range(n)]


def _plan(T, topo):
    cores = list(T.cores)
    P, Q = cores[:NP_], cores[NP_:]
    chips = []
    for c in Q:
        if topo.chip(c) not in chips:
            chips.append(topo.chip(c))
    takes, team = {}, {}
    for ch in chips:
        qs = [c for c in Q if topo.chip(c) == ch]
        for d in sorted(set(topo.die(c) for c in qs)):
            for p, c in zip([p for p in range(NP_) if topo.die(P[p]) == d], [c for c in qs if topo.die(c) == d]):
                takes[c], team[c] = p, qs
        assert sorted(takes[c] for c in qs) == list(range(NP_))
    return P, Q, chips, takes, team


def _dst(topo, c):
    rid, pid, _ = topo.addr(c)
    return DstId(rid=rid, pnc=pid)


def _h_groups(topo, src, Q, chips):
    common = -1
    for c in Q:
        common &= topo.mask(src, c)
    return _split(_engines(common), len(chips))


def _program_p(g, core, T, topo, p, Q, chips, takes):
    s = T.sem
    g.sync.dma_start(T.xs[:], T.x[:]).then_inc(s.lx, 16)
    g.scalar.dma_start(T.w1s[:], T.w1[:]).then_inc(s.lw1, 16)
    g.vector.memset(T.zero[:], 0.0).then_inc(s.zs, 1)

    g.tensor.wait_ge(s.lw1, 16)
    g.tensor.wait_ge(s.lx, 16)
    g.tensor.matmul(T.ps0[:, 0:TK], T.w1s[:], T.xs[:], True, True).then_inc(s.m1, 1)

    g.vector.wait_ge(s.zs, 1)
    g.vector.wait_ge(s.m1, 1)
    g.vector.tensor_tensor(T.hs[:], T.ps0[:, 0:TK], T.zero[:], AluOpType.max).then_inc(s.hr, 1)

    transfers, total = [], 0
    for ch, engs in zip(chips, _h_groups(topo, core, Q, chips)):
        (c,) = [c for c in Q if topo.chip(c) == ch and takes[c] == p]
        assert topo.may_write(core, c)
        transfers.append(RemoteDMATransfer(
            dst_ids=[_dst(topo, c)], dma_engine_mask=_mask(engs), remote_sem=s.ha0,
            srcs=[T.hs[:]], dsts=[T.hin[:, 0:TK]]))
        total += len(engs)
    g.wait_ge(s.hr, 1)
    g.remote_dma_fused(transfers, local_sem=s.sent)
    g.wait_ge(s.sent, total)


def _program_q(g, core, T, topo, takes, team, h_inc):
    s = T.sem
    near = [c for c in team[core] if topo.die(c) == topo.die(core)]
    far = [c for c in team[core] if topo.die(c) != topo.die(core)]
    (partner,) = [c for c in near if c != core]
    me_p = takes[core]

    def tile(p):
        return T.w2s[:, p * D:(p + 1) * D]

    def slot(k):
        return T.hin[:, k * TK:(k + 1) * TK]

    g.sync.dma_start(T.w2s[:], T.w2[:]).then_inc(s.lw, 16)

    rid, pid, _ = topo.addr(partner)
    pmask = topo.mask(core, partner)
    n_p = len(_engines(pmask))
    fmask = -1
    for c in far:
        fmask &= topo.mask(core, c)
    n_f = len(_engines(fmask))
    g.wait_ge(s.lw, 16)
    g.remote_dma(out_ap=T.wsib[:], in_ap=tile(takes[partner]), remote_sem=s.warr, local_sem=s.sent,
                 pid=pid, routing_id=rid, dma_engine_mask=pmask)
    k = 1 + near.index(core)
    g.wait_ge(s.ha0, h_inc)
    g.remote_dma_fused([RemoteDMATransfer(
        dst_ids=[_dst(topo, c) for c in far], dma_engine_mask=fmask, remote_sem=s["ha%d" % k],
        srcs=[slot(0)], dsts=[slot(k) for c in far])], local_sem=s.sent)
    g.wait_ge(s.cp, 1)
    g.remote_dma(out_ap=T.rb[:], in_ap=T.sb[:], remote_sem=s.pa, local_sem=s.sent,
                 pid=pid, routing_id=rid, dma_engine_mask=pmask)
    g.wait_ge(s.sent, 2 * n_p + n_f)

    g.tensor.wait_ge(s.warr, len(_engines(topo.mask(partner, core))))
    g.tensor.wait_ge(s.ha0, h_inc)
    g.tensor.matmul(T.ps1[:, 0:TK], T.wsib[:], slot(0), True, True).then_inc(s.pm1, 1)
    g.tensor.wait_ge(s.lw, 16)
    g.tensor.matmul(T.ps0[:, 0:TK], tile(me_p), slot(0), True, False)
    for i, c in enumerate(far):
        g.tensor.wait_ge(s["ha%d" % (1 + i)], len(_engines(topo.mask(c, core))))
        mm = g.tensor.matmul(T.ps0[:, 0:TK], tile(takes[c]), slot(1 + i), False, i == len(far) - 1)
    mm.then_inc(s.pm0, 1)

    g.vector.wait_ge(s.pm1, 1)
    g.vector.tensor_copy(T.sb[:], T.ps1[:, 0:TK]).then_inc(s.cp, 1)
    g.vector.wait_ge(s.pa, len(_engines(topo.mask(partner, core))))
    g.vector.wait_ge(s.pm0, 1)
    g.vector.tensor_tensor(T.ysb[:], T.ps0[:, 0:TK], T.rb[:], AluOpType.add).then_inc(s.fin, 1)

    g.sync.wait_ge(s.fin, 1)
    g.sync.dma_start(T.y[:], T.ysb[:]).then_inc(s.st, 16)
    g.sync.wait_ge(s.st, 16)


def rank_program(g, core, T, topo):
    rank = T.rank_of(core)
    if rank is None:
        return
    P, Q, chips, takes, team = _plan(T, topo)
    if rank < NP_:
        _program_p(g, core, T, topo, rank, Q, chips, takes)
    else:
        h_inc = len(_h_groups(topo, P[takes[core]], Q, chips)[0])
        _program_q(g, core, T, topo, takes, team, h_inc)
